import numpy as np
import ml_dtypes


def mxq(x, axis, fmt="e4m3"):
    dtype, down = {"e4m3": (ml_dtypes.float8_e4m3fn, 7), "e5m2": (ml_dtypes.float8_e5m2, 14)}[fmt]
    v = np.moveaxis(np.asarray(x, np.float32).astype(ml_dtypes.bfloat16).astype(np.float64), axis, -1)
    blocks = v.reshape(v.shape[:-1] + (-1, 32))
    amax = np.abs(blocks).max(-1, keepdims=True)
    byte = np.maximum(np.where(amax > 0, np.frexp(amax)[1] - 1 + 127, 0) - down, 1)
    scale = np.exp2(byte - 127.0)
    codes = (blocks / scale).astype(np.float32).astype(dtype).astype(np.float64)
    return np.moveaxis((codes * scale).reshape(v.shape), -1, axis)


WIDE = False


def mx_kscale(k):
    if not WIDE:
        return np.ones(k)
    levels = np.array([10, -10, 5, -5, 0])
    if k % 512:
        return np.exp2(np.random.permutation(np.resize(levels, k // 32))).repeat(32)
    a = np.empty((k // 512, 16))
    for p in range(k // 512):
        a[p, :8] = np.random.permutation(np.resize(levels, 8))
        for g in range(8):
            far = levels[np.abs(levels - a[p, g]) >= 10]
            a[p, g + 8] = far[np.random.randint(len(far))]
    return np.exp2(a.ravel()).repeat(32)


def f64(x):
    return np.asarray(x).astype(np.float64)


def striped(idx):
    return np.tile(idx.reshape(-1, 16).T, (8, 1)).astype(np.uint16)


def unstriped(offs):
    return offs[:16].T.reshape(-1).astype(np.int64)


K, T, E, C, N = 128, 768, 12, 256, 1536
TOP = 4


def by_expert(wq, xq):
    return np.concatenate([wq[e].T @ xq[:, e * C:(e + 1) * C] for e in range(E)], axis=1)


def setup_inputs():
    n = np.random.standard_normal
    s = mx_kscale(N)[:, None]
    deal = np.repeat(np.arange(E), C).reshape(TOP, T)[:, np.random.permutation(T)]
    deal = np.take_along_axis(deal, np.argsort(np.random.rand(TOP, T), axis=0), axis=0)
    for _ in range(8):
        s_, t_ = np.random.permutation(T).reshape(2, -1); r = np.random.randint(TOP, size=T // 2); x, y = deal[r, s_].copy(), deal[r, t_].copy()
        ok = ~((deal[:, s_] == y).any(0) | (deal[:, t_] == x).any(0)); deal[r[ok], s_[ok]] = y[ok]; deal[r[ok], t_[ok]] = x[ok]
    order = np.lexsort((np.random.rand(TOP * T), deal.reshape(-1)))
    slot_token = order % T; pos = np.empty(TOP * T, np.int64); pos[order] = np.arange(TOP * T); pos = pos.reshape(TOP, T)
    g = np.random.uniform(0.5, 1.5, (TOP, T)); g = g / g.sum(0)
    w_slot = np.empty(E * C)
    for r in range(TOP): w_slot[pos[r]] = g[r]
    return {
        "dyT": (n((N, T)) * s).astype(np.float32),
        "w": (n((E, N, K)) / np.sqrt(N) / s[None]).astype(np.float32),
        "gate": np.tile(w_slot, (N, 1)).astype(np.float32),
        "offs": striped(slot_token),
        "pos1": striped(pos[0]),
        "pos2": striped(pos[1]),
        "pos3": striped(pos[2]),
        "pos4": striped(pos[3]),
    }


def reference(dyT, w, gate, offs, pos1, pos2, pos3, pos4):
    idx = unstriped(offs)
    gq = mxq(f64(gate) * f64(dyT)[:, idx], 0, "e4m3")
    dx = by_expert(mxq(f64(w), 1, "e4m3"), gq)
    return dx[:, unstriped(pos1)] + dx[:, unstriped(pos2)] + dx[:, unstriped(pos3)] + dx[:, unstriped(pos4)]

@@ -1,0 +1,205 @@
+from contextlib import ExitStack
+
+import concourse.mybir as mybir
+from concourse.masks import make_identity
+
+K, T, E, C, N = 128, 768, 12, 256, 1536
+S = E * C
+FLOPS = 2 * S * N * K
+BYTES = 4 * (N * T + E * N * K + S + K * T) + 2 * 128 * (S + 4 * T) // 16
+
+F32 = mybir.dt.float32
+BF16 = mybir.dt.bfloat16
+U32 = mybir.dt.uint32
+U16 = mybir.dt.uint16
+U8 = mybir.dt.uint8
+FP8X4 = mybir.dt.float8_e4m3fn_x4
+MULT = mybir.AluOpType.mult
+ADD = mybir.AluOpType.add
+COPY = mybir.ActivationFunctionType.Copy
+
+P = 128
+PACK = 4
+PASSES = N // (P * PACK)
+CH = 2 * C
+NCH = S // CH
+V_CHUNK = 1
+AHEAD = 4
+W_BUFS = 5
+OUT_WIDTHS = (128, 384, 256)
+
+
+def tile_moe_bdx_lin_none_kernel(tc, dyT, w, gate, offs, pos1, pos2, pos3, pos4, out):
+    nc = tc.nc
+    with ExitStack() as ctx:
+        keep = ctx.enter_context(tc.tile_pool(name="keep", bufs=1))
+        ring = ctx.enter_context(tc.tile_pool(name="ring", bufs=2))
+        psum = ctx.enter_context(tc.psum_pool(name="psum", bufs=2))
+
+        v_units = [(2, 2, 0), (2, 2, 1)]
+        s_units = [(2 * c, 2, a) for c in range(NCH) for a in range(PASSES) if (2 * c, 2, a) not in v_units][:-1] + [(E - 2, 1, PASSES - 1), (E - 1, 1, PASSES - 1)]
+        v_lo = min(u[0] for u in v_units) * C
+        v_hi = max(u[0] + u[1] for u in v_units) * C
+
+        offs_sb = keep.tile([P, S // 16], U16, name="offs_sb")
+        dy_rows = dyT.rearrange("(a p t) x -> a t p x", p=P, t=PACK)
+        dy = [[keep.tile([P, T], F32, name=f"dy{a}_{t}") for t in range(PACK)] for a in range(PASSES)]
+        gate_v = keep.tile([P, v_hi - v_lo], F32, name="gate_v")
+        gate_rows = keep.tile([P, P], F32, name="gate_rows")
+        nc.sync.dma_start(dy[0][0][:], dy_rows[0, 0])
+        nc.sync.dma_start(offs_sb[:], offs)
+        nc.sync.dma_start(gate_v[:], gate[0:P, v_lo:v_hi])
+        for t in range(1, PACK):
+            nc.sync.dma_start(dy[0][t][:], dy_rows[0, t])
+        nc.sync.dma_start(gate_rows[:], gate.rearrange("r (m q) -> (r m) q", q=P)[0:P, :])
+        for a in range(1, PASSES):
+            for t in range(PACK):
+                nc.sync.dma_start(dy[a][t][:], dy_rows[a, t])
+        pos_sb = []
+        for r, pos in enumerate((pos1, pos2, pos3, pos4)):
+            pos_tile = keep.tile([P, T // 16], U16, name=f"pos_sb{r}")
+            nc.sync.dma_start(pos_tile[:], pos)
+            pos_sb.append(pos_tile)
+
+        ident = keep.tile([P, P], F32, name="ident")
+        make_identity(nc, ident[:])
+        turned = psum.tile([P, P], F32, name="turned", tag="acc", bufs=5)
+        nc.tensor.transpose(turned[:], gate_rows[:], ident[:])
+        gate_cols = keep.tile([P, S // P], F32, name="gate_cols")
+        nc.vector.tensor_copy(gate_cols[:], turned[:, 0:S // P])
+
+        dx = keep.tile([P, S], F32, name="dx")
+        gate_ps, planes, g_bf, g_mx, w_raw, w_bf, w_mx, acc = {}, {}, {}, {}, {}, {}, {}, {}
+
+        def spread_gate(c):
+            bank = psum.tile([P, CH], F32, name="gate_bank", bufs=3)
+            for b in range(CH // P):
+                m = c * (CH // P) + b
+                nc.tensor.transpose(bank[:, b * P:(b + 1) * P], gate_cols[:, m:m + 1].to_broadcast([P, P]), ident[:])
+            gate_ps[c] = bank
+
+        def slots(u):
+            return offs_sb[:, u[0] * C // 16:(u[0] + u[1]) * C // 16]
+
+        def gather_scalar(u):
+            planes[u] = ring.tile([P, PACK, u[1] * C], F32, name="planes_s", bufs=AHEAD + 1)
+            for t in range(PACK):
+                nc.scalar.activation(planes[u][:, t, :], dy[u[2]][t][:].indirect(slots(u)), COPY)
+
+        def gather_vector(u):
+            planes[u] = ring.tile([P, PACK, u[1] * C], F32, name="planes_v", bufs=2)
+            gates = gate_v[:, u[0] * C - v_lo:(u[0] + u[1]) * C - v_lo]
+            for t in range(PACK):
+                nc.vector.tensor_tensor(planes[u][:, t, :], dy[u[2]][t][:].indirect(slots(u)), gates, MULT)
+
+        def weave(u):
+            g_bf[u] = ring.tile([P, u[1] * C, PACK], BF16, name="g_bf", bufs=3, align_bytes=64)
+            nc.vector.tensor_copy(
+                g_bf[u][:].rearrange("p (x i) t -> p x t i", i=4),
+                planes[u][:].rearrange("p t (x i) -> p x t i", i=4))
+
+        def gate_and_weave(u):
+            n = u[1] * C
+            g_bf[u] = ring.tile([P, n, PACK], BF16, name="g_bf", bufs=3, align_bytes=64)
+            first = (u[0] % 2) * C
+            gates = gate_ps[u[0] // 2][:, first:first + n]
+            nc.vector.tensor_tensor(
+                g_bf[u][:].rearrange("p (x i) t -> p x t i", i=2),
+                planes[u][:].rearrange("p t (x i) -> p x t i", i=2),
+                gates.rearrange("p (x i) -> p x i", i=2).unsqueeze(2).to_broadcast([P, n // 2, PACK, 2]),
+                MULT)
+
+        def quantize_g(u):
+            codes = ring.tile([P, u[1] * C], U32, name="g_codes", bufs=10, align_bytes=64)
+            scales = ring.tile([P, u[1] * C], U8, name="g_scales", bufs=10, align_bytes=64)
+            nc.vector.quantize_mx(out=codes[:].bitcast(FP8X4), scales=scales[:],
+                                  in_=g_bf[u][:].rearrange("p x t -> p (x t)"))
+            for h in range(u[1]):
+                g_mx[u[0] + h, u[2]] = (codes[:, h * C:(h + 1) * C], scales[:, h * C:(h + 1) * C])
+
+        def load_w(e):
+            w_raw[e] = ring.tile([P, PASSES, PACK, K], F32, name="w_raw", bufs=W_BUFS)
+            nc.sync.dma_start(w_raw[e][:], w[e].rearrange("(a p j) k -> p a j k", p=P, j=PACK))
+
+        def weave_w(e):
+            w_bf[e] = ring.tile([P, PASSES, K, PACK], BF16, name="w_bf", bufs=2, align_bytes=64)
+            nc.vector.tensor_copy(
+                w_bf[e][:].rearrange("p a (x i) j -> p x a j i", i=4),
+                w_raw[e][:].rearrange("p a j (x i) -> p x a j i", i=4))
+
+        def quantize_w(e):
+            codes = ring.tile([P, PASSES * K], U32, name="w_codes", bufs=5, align_bytes=64)
+            scales = ring.tile([P, PASSES * K], U8, name="w_scales", bufs=5, align_bytes=64)
+            nc.vector.quantize_mx(out=codes[:].bitcast(FP8X4), scales=scales[:],
+                                  in_=w_bf[e][:].rearrange("p a k j -> p (a k j)"))
+            w_mx[e] = (codes, scales)
+
+        def multiply(e, a):
+            if a == 0:
+                acc[e] = psum.tile([P, C], F32, name="acc", tag="acc", bufs=5)
+            nc.tensor.matmul_mx(
+                out=acc[e][:],
+                lhsT=w_mx[e][0][:, a * K:(a + 1) * K].bitcast(FP8X4),
+                lhsT_scale=w_mx[e][1][:, a * K:(a + 1) * K],
+                rhs=g_mx[e, a][0].bitcast(FP8X4),
+                rhs_scale=g_mx[e, a][1],
+                start=(a == 0), stop=(a == PASSES - 1))
+            if a == PASSES - 1:
+                if e % 2 == 0:
+                    nc.vector.tensor_copy(dx[:, e * C:(e + 1) * C], acc[e][:])
+                else:
+                    nc.scalar.copy(dx[:, e * C:(e + 1) * C], acc[e][:])
+
+        for e in range(W_BUFS):
+            load_w(e)
+        spread_gate(0)
+        spread_gate(1)
+        for i in range(AHEAD):
+            gather_scalar(s_units[i])
+        for i, u in enumerate(v_units):
+            gather_vector(u)
+            if i >= 1:
+                weave(v_units[i - 1])
+            if i >= 2:
+                quantize_g(v_units[i - 2])
+        weave(v_units[-1])
+        for u in v_units[-2:]:
+            quantize_g(u)
+
+        passes_done = [0] * E
+        for s in range(len(s_units) + 1):
+            if s + AHEAD < len(s_units):
+                gather_scalar(s_units[s + AHEAD])
+            if s < len(s_units):
+                c = s_units[s][0] // 2
+                if c + 1 < NCH and c + 1 not in gate_ps:
+                    spread_gate(c + 1)
+                gate_and_weave(s_units[s])
+            if s < E:
+                weave_w(s)
+                if s + W_BUFS < E:
+                    load_w(s + W_BUFS)
+            if s >= 1:
+                quantize_g(s_units[s - 1])
+            if 1 <= s <= E:
+                quantize_w(s - 1)
+            for e in range(E):
+                while passes_done[e] < PASSES and e in w_mx and (e, passes_done[e]) in g_mx and (e < 2 or passes_done[e - 2] == PASSES):
+                    multiply(e, passes_done[e])
+                    passes_done[e] += 1
+
+        first_token = 0
+        for width in OUT_WIDTHS:
+            cols = slice(first_token // 16, (first_token + width) // 16)
+            first = ring.tile([P, width], F32, name="first", bufs=3)
+            second = ring.tile([P, width], F32, name="second", bufs=3)
+            nc.scalar.activation(first[:], dx[:].indirect(pos_sb[0][:, cols]), COPY)
+            nc.scalar.activation(second[:], dx[:].indirect(pos_sb[1][:, cols]), COPY)
+            two = ring.tile([P, width], F32, name="two", bufs=2)
+            three = ring.tile([P, width], F32, name="three", bufs=2)
+            four = ring.tile([P, width], F32, name="four", bufs=3)
+            nc.vector.tensor_tensor(two[:], dx[:].indirect(pos_sb[2][:, cols]), first[:], ADD)
+            nc.vector.tensor_tensor(three[:], dx[:].indirect(pos_sb[3][:, cols]), two[:], ADD)
+            nc.vector.tensor_tensor(four[:], three[:], second[:], ADD)
+            nc.sync.dma_start(out[:, first_token:first_token + width], four[:])
+            first_token += width

@@ -24,7 +24,7 @@ PASSES = N // (P * PACK)
 CH = 2 * C
 NCH = S // CH
 V_CHUNK = 1
-AHEAD = 4
+AHEAD = 5
 W_BUFS = 5
 OUT_WIDTHS = (128, 384, 256)
 
@@ -36,8 +36,8 @@ def tile_moe_bdx_lin_none_kernel(tc, dyT, w, gate, offs, pos1, pos2, pos3, pos4,
         ring = ctx.enter_context(tc.tile_pool(name="ring", bufs=2))
         psum = ctx.enter_context(tc.psum_pool(name="psum", bufs=2))
 
-        v_units = [(2, 2, 0), (2, 2, 1)]
-        s_units = [(2 * c, 2, a) for c in range(NCH) for a in range(PASSES) if (2 * c, 2, a) not in v_units][:-1] + [(E - 2, 1, PASSES - 1), (E - 1, 1, PASSES - 1)]
+        v_units = [(2, 2, 0), (4, 1, 0), (2, 2, 1), (2, 2, 2)]
+        s_units = [(0, 2, 0), (0, 2, 1), (0, 2, 2), (5, 1, 0)] + [(2 * c, 2, a) for c in range(2, NCH) for a in range(PASSES)][1:-1] + [(E - 2, 1, PASSES - 1), (E - 1, 1, PASSES - 1)]
         v_lo = min(u[0] for u in v_units) * C
         v_hi = max(u[0] + u[1] for u in v_units) * C
 
@@ -93,7 +93,10 @@ def tile_moe_bdx_lin_none_kernel(tc, dyT, w, gate, offs, pos1, pos2, pos3, pos4,
                 nc.vector.tensor_tensor(planes[u][:, t, :], dy[u[2]][t][:].indirect(slots(u)), gates, MULT)
 
         def weave(u):
-            g_bf[u] = ring.tile([P, u[1] * C, PACK], BF16, name="g_bf", bufs=3, align_bytes=64)
+            if u == v_units[-1]:
+                g_bf[u] = ring.tile([P, u[1] * C, PACK], BF16, name="w_bf", tag="w_bf", bufs=1, align_bytes=64)
+            else:
+                g_bf[u] = ring.tile([P, u[1] * C, PACK], BF16, name="g_bf", bufs=3, align_bytes=64)
             nc.vector.tensor_copy(
                 g_bf[u][:].rearrange("p (x i) t -> p x t i", i=4),
                 planes[u][:].rearrange("p t (x i) -> p x t i", i=4))
@@ -110,8 +113,8 @@ def tile_moe_bdx_lin_none_kernel(tc, dyT, w, gate, offs, pos1, pos2, pos3, pos4,
                 MULT)
 
         def quantize_g(u):
-            codes = ring.tile([P, u[1] * C], U32, name="g_codes", bufs=10, align_bytes=64)
-            scales = ring.tile([P, u[1] * C], U8, name="g_scales", bufs=10, align_bytes=64)
+            codes = ring.tile([P, u[1] * C], U32, name="g_codes", bufs=12, align_bytes=64)
+            scales = ring.tile([P, u[1] * C], U8, name="g_scales", bufs=12, align_bytes=64)
             nc.vector.quantize_mx(out=codes[:].bitcast(FP8X4), scales=scales[:],
                                   in_=g_bf[u][:].rearrange("p x t -> p (x t)"))
             for h in range(u[1]):
@@ -122,10 +125,8 @@ def tile_moe_bdx_lin_none_kernel(tc, dyT, w, gate, offs, pos1, pos2, pos3, pos4,
             nc.sync.dma_start(w_raw[e][:], w[e].rearrange("(a p j) k -> p a j k", p=P, j=PACK))
 
         def weave_w(e):
-            w_bf[e] = ring.tile([P, PASSES, K, PACK], BF16, name="w_bf", bufs=2, align_bytes=64)
-            nc.vector.tensor_copy(
-                w_bf[e][:].rearrange("p a (x i) j -> p x a j i", i=4),
-                w_raw[e][:].rearrange("p a j (x i) -> p x a j i", i=4))
+            w_bf[e] = ring.tile([P, PASSES, K, PACK], BF16, name="w_bf", tag="w_bf", bufs=1, align_bytes=64)
+            nc.gpsimd.tensor_scalar(w_bf[e][:], w_raw[e][:].rearrange("p a j k -> p a k j"), 1.0, 0.0, MULT, ADD)
 
         def quantize_w(e):
             codes = ring.tile([P, PASSES * K], U32, name="w_codes", bufs=5, align_bytes=64)
@@ -153,7 +154,6 @@ def tile_moe_bdx_lin_none_kernel(tc, dyT, w, gate, offs, pos1, pos2, pos3, pos4,
         for e in range(W_BUFS):
             load_w(e)
         spread_gate(0)
-        spread_gate(1)
         for i in range(AHEAD):
             gather_scalar(s_units[i])
         for i, u in enumerate(v_units):
@@ -172,21 +172,26 @@ def tile_moe_bdx_lin_none_kernel(tc, dyT, w, gate, offs, pos1, pos2, pos3, pos4,
                 gather_scalar(s_units[s + AHEAD])
             if s < len(s_units):
                 c = s_units[s][0] // 2
-                if c + 1 < NCH and c + 1 not in gate_ps:
-                    spread_gate(c + 1)
+                for later in range(c + 1, min(c + 3, NCH)):
+                    if later != V_CHUNK and later not in gate_ps:
+                        spread_gate(later)
+                        break
                 gate_and_weave(s_units[s])
-            if s < E:
-                weave_w(s)
-                if s + W_BUFS < E:
-                    load_w(s + W_BUFS)
-            if s >= 1:
-                quantize_g(s_units[s - 1])
-            if 1 <= s <= E:
-                quantize_w(s - 1)
             for e in range(E):
                 while passes_done[e] < PASSES and e in w_mx and (e, passes_done[e]) in g_mx and (e < 2 or passes_done[e - 2] == PASSES):
                     multiply(e, passes_done[e])
                     passes_done[e] += 1
+            if s >= 1:
+                quantize_g(s_units[s - 1])
+            if 1 <= s <= E:
+                quantize_w(s - 1)
+            if s < E:
+                weave_w(s)
+                if s + W_BUFS < E:
+                    load_w(s + W_BUFS)
+        for e in range(E):
+            for a in range(passes_done[e], PASSES):
+                multiply(e, a)
 
         first_token = 0
         for width in OUT_WIDTHS:

@@ -21,12 +21,11 @@ COPY = mybir.ActivationFunctionType.Copy
 P = 128
 PACK = 4
 PASSES = N // (P * PACK)
-CH = 2 * C
-NCH = S // CH
-V_CHUNK = 1
-AHEAD = 5
-W_BUFS = 5
-OUT_WIDTHS = (128, 384, 256)
+BANK = 512
+WINDOW = 1040
+PLANE_BUFS = 4
+W_BUFS = 4
+G_BUFS = 11
 
 
 def tile_moe_bdx_lin_none_kernel(tc, dyT, w, gate, offs, pos1, pos2, pos3, pos4, out):
@@ -36,25 +35,30 @@ def tile_moe_bdx_lin_none_kernel(tc, dyT, w, gate, offs, pos1, pos2, pos3, pos4,
         ring = ctx.enter_context(tc.tile_pool(name="ring", bufs=2))
         psum = ctx.enter_context(tc.psum_pool(name="psum", bufs=2))
 
-        v_units = [(2, 2, 0), (4, 1, 0), (2, 2, 1), (2, 2, 2)]
-        s_units = [(0, 2, 0), (0, 2, 1), (0, 2, 2), (5, 1, 0)] + [(2 * c, 2, a) for c in range(2, NCH) for a in range(PASSES)][1:-1] + [(E - 2, 1, PASSES - 1), (E - 1, 1, PASSES - 1)]
-        v_lo = min(u[0] for u in v_units) * C
-        v_hi = max(u[0] + u[1] for u in v_units) * C
+        v_runs = [(0, 768, 0), (0, 512, 1), (0, 512, 2)]
+        s_runs = [(768, 768, 0), (512, 1024, 1), (512, 1024, 2), (1536, 1024, 0), (1536, 1024, 1), (1536, 1024, 2), (2560, 512, 0), (2560, 512, 1), (2560, 256, 2), (2816, 128, 2), (2944, 128, 2)]
+        v_slots = max(r[0] + r[1] for r in v_runs)
+
+        def pieces(run):
+            first, count, a = run
+            cuts = sorted({first, first + count} | {b for b in range(0, S, BANK) if first < b < first + count})
+            return [(lo, hi - lo, a) for lo, hi in zip(cuts, cuts[1:])]
 
         offs_sb = keep.tile([P, S // 16], U16, name="offs_sb")
         dy_rows = dyT.rearrange("(a p t) x -> a t p x", p=P, t=PACK)
-        dy = [[keep.tile([P, T], F32, name=f"dy{a}_{t}") for t in range(PACK)] for a in range(PASSES)]
-        gate_v = keep.tile([P, v_hi - v_lo], F32, name="gate_v")
+        dy = [[keep.tile([P, WINDOW], F32, name=f"dy{a}_{t}") for t in range(PACK)] for a in range(PASSES)]
+        gate_v = keep.tile([P, v_slots], F32, name="gate_v")
         gate_rows = keep.tile([P, P], F32, name="gate_rows")
-        nc.sync.dma_start(dy[0][0][:], dy_rows[0, 0])
+
         nc.sync.dma_start(offs_sb[:], offs)
-        nc.sync.dma_start(gate_v[:], gate[0:P, v_lo:v_hi])
+        nc.sync.dma_start(dy[0][0][:, 0:T], dy_rows[0, 0])
+        nc.sync.dma_start(gate_v[:], gate[0:P, 0:v_slots])
         for t in range(1, PACK):
-            nc.sync.dma_start(dy[0][t][:], dy_rows[0, t])
+            nc.sync.dma_start(dy[0][t][:, 0:T], dy_rows[0, t])
         nc.sync.dma_start(gate_rows[:], gate.rearrange("r (m q) -> (r m) q", q=P)[0:P, :])
         for a in range(1, PASSES):
             for t in range(PACK):
-                nc.sync.dma_start(dy[a][t][:], dy_rows[a, t])
+                nc.sync.dma_start(dy[a][t][:, 0:T], dy_rows[a, t])
         pos_sb = []
         for r, pos in enumerate((pos1, pos2, pos3, pos4)):
             pos_tile = keep.tile([P, T // 16], U16, name=f"pos_sb{r}")
@@ -72,53 +76,56 @@ def tile_moe_bdx_lin_none_kernel(tc, dyT, w, gate, offs, pos1, pos2, pos3, pos4,
         gate_ps, planes, g_bf, g_mx, w_raw, w_bf, w_mx, acc = {}, {}, {}, {}, {}, {}, {}, {}
 
         def spread_gate(c):
-            bank = psum.tile([P, CH], F32, name="gate_bank", bufs=3)
-            for b in range(CH // P):
-                m = c * (CH // P) + b
-                nc.tensor.transpose(bank[:, b * P:(b + 1) * P], gate_cols[:, m:m + 1].to_broadcast([P, P]), ident[:])
-            gate_ps[c] = bank
+            gate_ps[c] = psum.tile([P, BANK], F32, name="gate_bank", bufs=3)
+            for b in range(BANK // P):
+                m = c * (BANK // P) + b
+                nc.tensor.transpose(gate_ps[c][:, b * P:(b + 1) * P], gate_cols[:, m:m + 1].to_broadcast([P, P]), ident[:])
 
-        def slots(u):
-            return offs_sb[:, u[0] * C // 16:(u[0] + u[1]) * C // 16]
+        def offsets(run):
+            return offs_sb[:, run[0] // 16:(run[0] + run[1]) // 16]
 
-        def gather_scalar(u):
-            planes[u] = ring.tile([P, PACK, u[1] * C], F32, name="planes_s", bufs=AHEAD + 1)
+        def hand_on(run, tile):
+            for piece in pieces(run):
+                planes[piece] = tile[:, :, piece[0] - run[0]:piece[0] - run[0] + piece[1]]
+
+        def gather_scalar(run):
+            tile = ring.tile([P, PACK, run[1]], F32, name="planes_s", tag="planes_s", bufs=PLANE_BUFS)
             for t in range(PACK):
-                nc.scalar.activation(planes[u][:, t, :], dy[u[2]][t][:].indirect(slots(u)), COPY)
+                nc.scalar.activation(tile[:, t, :], dy[run[2]][t][:].indirect(offsets(run)), COPY)
+            hand_on(run, tile)
 
-        def gather_vector(u):
-            planes[u] = ring.tile([P, PACK, u[1] * C], F32, name="planes_v", bufs=2)
-            gates = gate_v[:, u[0] * C - v_lo:(u[0] + u[1]) * C - v_lo]
+        def gather_vector(run):
+            tile = ring.tile([P, PACK, run[1]], F32, name="planes_v", bufs=2)
             for t in range(PACK):
-                nc.vector.tensor_tensor(planes[u][:, t, :], dy[u[2]][t][:].indirect(slots(u)), gates, MULT)
+                nc.vector.tensor_tensor(tile[:, t, :], dy[run[2]][t][:].indirect(offsets(run)),
+                                        gate_v[:, run[0]:run[0] + run[1]], MULT)
+            hand_on(run, tile)
 
-        def weave(u):
-            if u == v_units[-1]:
-                g_bf[u] = ring.tile([P, u[1] * C, PACK], BF16, name="w_bf", tag="w_bf", bufs=1, align_bytes=64)
-            else:
-                g_bf[u] = ring.tile([P, u[1] * C, PACK], BF16, name="g_bf", bufs=3, align_bytes=64)
+        def weave(piece, tag, bufs):
+            g_bf[piece] = ring.tile([P, piece[1], PACK], BF16, name=tag, tag=tag, bufs=bufs, align_bytes=64)
             nc.vector.tensor_copy(
-                g_bf[u][:].rearrange("p (x i) t -> p x t i", i=4),
-                planes[u][:].rearrange("p t (x i) -> p x t i", i=4))
+                g_bf[piece][:].rearrange("p (x i) t -> p x t i", i=4),
+                planes[piece].rearrange("p t (x i) -> p x t i", i=4))
 
-        def gate_and_weave(u):
-            n = u[1] * C
-            g_bf[u] = ring.tile([P, n, PACK], BF16, name="g_bf", bufs=3, align_bytes=64)
-            first = (u[0] % 2) * C
-            gates = gate_ps[u[0] // 2][:, first:first + n]
+        def gate_and_weave(piece):
+            first, count, a = piece
+            g_bf[piece] = ring.tile([P, count, PACK], BF16, name="g_bf", tag="g_bf", bufs=3, align_bytes=64)
+            gates = gate_ps[first // BANK][:, first % BANK:first % BANK + count]
             nc.vector.tensor_tensor(
-                g_bf[u][:].rearrange("p (x i) t -> p x t i", i=2),
-                planes[u][:].rearrange("p t (x i) -> p x t i", i=2),
-                gates.rearrange("p (x i) -> p x i", i=2).unsqueeze(2).to_broadcast([P, n // 2, PACK, 2]),
+                g_bf[piece][:].rearrange("p (x i) t -> p x t i", i=2),
+                planes[piece].rearrange("p t (x i) -> p x t i", i=2),
+                gates.rearrange("p (x i) -> p x i", i=2).unsqueeze(2).to_broadcast([P, count // 2, PACK, 2]),
                 MULT)
 
-        def quantize_g(u):
-            codes = ring.tile([P, u[1] * C], U32, name="g_codes", bufs=12, align_bytes=64)
-            scales = ring.tile([P, u[1] * C], U8, name="g_scales", bufs=12, align_bytes=64)
+        def quantize_g(piece):
+            first, count, a = piece
+            codes = ring.tile([P, count], U32, name="g_codes", bufs=G_BUFS, align_bytes=64)
+            scales = ring.tile([P, count], U8, name="g_scales", bufs=G_BUFS, align_bytes=64)
             nc.vector.quantize_mx(out=codes[:].bitcast(FP8X4), scales=scales[:],
-                                  in_=g_bf[u][:].rearrange("p x t -> p (x t)"))
-            for h in range(u[1]):
-                g_mx[u[0] + h, u[2]] = (codes[:, h * C:(h + 1) * C], scales[:, h * C:(h + 1) * C])
+                                  in_=g_bf[piece][:].rearrange("p x t -> p (x t)"))
+            for lo in range(0, count, C):
+                hi = min(lo + C, count)
+                g_mx.setdefault(((first + lo) // C, a), []).append((codes[:, lo:hi], scales[:, lo:hi], (first + lo) % C, hi - lo))
 
         def load_w(e):
             w_raw[e] = ring.tile([P, PASSES, PACK, K], F32, name="w_raw", bufs=W_BUFS)
@@ -135,76 +142,95 @@ def tile_moe_bdx_lin_none_kernel(tc, dyT, w, gate, offs, pos1, pos2, pos3, pos4,
                                   in_=w_bf[e][:].rearrange("p a k j -> p (a k j)"))
             w_mx[e] = (codes, scales)
 
+        def quantized(e, a):
+            return sum(part[3] for part in g_mx.get((e, a), [])) == C
+
         def multiply(e, a):
             if a == 0:
                 acc[e] = psum.tile([P, C], F32, name="acc", tag="acc", bufs=5)
-            nc.tensor.matmul_mx(
-                out=acc[e][:],
-                lhsT=w_mx[e][0][:, a * K:(a + 1) * K].bitcast(FP8X4),
-                lhsT_scale=w_mx[e][1][:, a * K:(a + 1) * K],
-                rhs=g_mx[e, a][0].bitcast(FP8X4),
-                rhs_scale=g_mx[e, a][1],
-                start=(a == 0), stop=(a == PASSES - 1))
+            parts = g_mx[e, a]
+            for i, (codes, scales, lo, count) in enumerate(parts):
+                nc.tensor.matmul_mx(
+                    out=acc[e][:, lo:lo + count],
+                    lhsT=w_mx[e][0][:, a * K:(a + 1) * K].bitcast(FP8X4),
+                    lhsT_scale=w_mx[e][1][:, a * K:(a + 1) * K],
+                    rhs=codes.bitcast(FP8X4),
+                    rhs_scale=scales,
+                    start=(a == 0), stop=(a == PASSES - 1 and i == len(parts) - 1))
             if a == PASSES - 1:
-                if e % 2 == 0:
+                if False:
                     nc.vector.tensor_copy(dx[:, e * C:(e + 1) * C], acc[e][:])
                 else:
                     nc.scalar.copy(dx[:, e * C:(e + 1) * C], acc[e][:])
 
+        s_pieces = [piece for run in s_runs for piece in pieces(run)]
+        v_pieces = [piece for run in v_runs for piece in pieces(run)]
+        s_banks = sorted({piece[0] // BANK for piece in s_pieces})
+
         for e in range(W_BUFS):
             load_w(e)
-        spread_gate(0)
-        for i in range(AHEAD):
-            gather_scalar(s_units[i])
-        for i, u in enumerate(v_units):
-            gather_vector(u)
+        for c in s_banks[:2]:
+            spread_gate(c)
+        for run in s_runs[:PLANE_BUFS - 1]:
+            gather_scalar(run)
+        gather_vector(v_runs[0])
+        for i, run in enumerate(v_runs):
+            if i + 1 < len(v_runs):
+                gather_vector(v_runs[i + 1])
+            for piece in pieces(run):
+                if piece == v_pieces[-1]:
+                    weave(piece, "w_bf", 1)
+                else:
+                    weave(piece, "g_bf", 3)
             if i >= 1:
-                weave(v_units[i - 1])
-            if i >= 2:
-                quantize_g(v_units[i - 2])
-        weave(v_units[-1])
-        for u in v_units[-2:]:
-            quantize_g(u)
+                for piece in pieces(v_runs[i - 1]):
+                    quantize_g(piece)
+        for piece in pieces(v_runs[-1]):
+            quantize_g(piece)
 
         passes_done = [0] * E
-        for s in range(len(s_units) + 1):
-            if s + AHEAD < len(s_units):
-                gather_scalar(s_units[s + AHEAD])
-            if s < len(s_units):
-                c = s_units[s][0] // 2
-                for later in range(c + 1, min(c + 3, NCH)):
-                    if later != V_CHUNK and later not in gate_ps:
-                        spread_gate(later)
-                        break
-                gate_and_weave(s_units[s])
+        gathered = PLANE_BUFS - 1
+        starts = [pieces(run)[0] for run in s_runs]
+        for s in range(len(s_pieces) + 2):
+            if s < len(s_pieces):
+                if s_pieces[s] in starts and gathered < len(s_runs):
+                    gather_scalar(s_runs[gathered])
+                    gathered += 1
+                for piece in s_pieces[s:s + 3]:
+                    if piece[0] // BANK not in gate_ps:
+                        spread_gate(piece[0] // BANK)
+                gate_and_weave(s_pieces[s])
             for e in range(E):
-                while passes_done[e] < PASSES and e in w_mx and (e, passes_done[e]) in g_mx and (e < 2 or passes_done[e - 2] == PASSES):
+                while passes_done[e] < PASSES and e in w_mx and quantized(e, passes_done[e]) and (e < 4 or passes_done[e - 4] == PASSES):
                     multiply(e, passes_done[e])
                     passes_done[e] += 1
-            if s >= 1:
-                quantize_g(s_units[s - 1])
+            if 1 <= s <= len(s_pieces):
+                quantize_g(s_pieces[s - 1])
             if 1 <= s <= E:
                 quantize_w(s - 1)
             if s < E:
                 weave_w(s)
                 if s + W_BUFS < E:
                     load_w(s + W_BUFS)
-        for e in range(E):
-            for a in range(passes_done[e], PASSES):
-                multiply(e, a)
+        assert passes_done == [PASSES] * E
 
-        first_token = 0
-        for width in OUT_WIDTHS:
-            cols = slice(first_token // 16, (first_token + width) // 16)
-            first = ring.tile([P, width], F32, name="first", bufs=3)
-            second = ring.tile([P, width], F32, name="second", bufs=3)
-            nc.scalar.activation(first[:], dx[:].indirect(pos_sb[0][:, cols]), COPY)
-            nc.scalar.activation(second[:], dx[:].indirect(pos_sb[1][:, cols]), COPY)
-            two = ring.tile([P, width], F32, name="two", bufs=2)
-            three = ring.tile([P, width], F32, name="three", bufs=2)
-            four = ring.tile([P, width], F32, name="four", bufs=3)
-            nc.vector.tensor_tensor(two[:], dx[:].indirect(pos_sb[2][:, cols]), first[:], ADD)
-            nc.vector.tensor_tensor(three[:], dx[:].indirect(pos_sb[3][:, cols]), two[:], ADD)
-            nc.vector.tensor_tensor(four[:], three[:], second[:], ADD)
-            nc.sync.dma_start(out[:, first_token:first_token + width], four[:])
-            first_token += width
+        spare = ring.tile([P, 5, T], F32, name="spare", tag="planes_s", bufs=PLANE_BUFS)
+        first, second, two, three, four = (spare[:, j, :] for j in range(5))
+
+        def picked(r, lo, hi):
+            return dx[:].indirect(pos_sb[r][:, lo // 16:hi // 16])
+
+        cuts = [(0, 128), (128, 384), (384, T)]
+        halves = [(0, 384), (384, T)]
+        for lo, hi in cuts:
+            nc.scalar.activation(first[:, lo:hi], picked(0, lo, hi), COPY)
+        for lo, hi in halves:
+            nc.scalar.activation(second[:, lo:hi], picked(1, lo, hi), COPY)
+        for kind, (lo, hi) in [(2, cuts[0]), (3, cuts[0]), (2, cuts[1]), (2, cuts[2]), (3, cuts[1]), (3, cuts[2])]:
+            if kind == 2:
+                nc.vector.tensor_tensor(two[:, lo:hi], picked(2, lo, hi), first[:, lo:hi], ADD)
+            else:
+                nc.vector.tensor_tensor(three[:, lo:hi], picked(3, lo, hi), two[:, lo:hi], ADD)
+        for lo, hi in halves:
+            nc.vector.tensor_tensor(four[:, lo:hi], three[:, lo:hi], second[:, lo:hi], ADD)
+            nc.sync.dma_start(out[:, lo:hi], four[:, lo:hi])

@@ -23,9 +23,10 @@ PACK = 4
 PASSES = N // (P * PACK)
 BANK = 512
 WINDOW = 1040
-PLANE_BUFS = 4
-W_BUFS = 4
-G_BUFS = 11
+PAIRS = E // 2
+PLANE_BUFS = 3
+W_BUFS = 2
+G_BUFS = 5
 
 
 def tile_moe_bdx_lin_none_kernel(tc, dyT, w, gate, offs, pos1, pos2, pos3, pos4, out):
@@ -35,26 +36,31 @@ def tile_moe_bdx_lin_none_kernel(tc, dyT, w, gate, offs, pos1, pos2, pos3, pos4,
         ring = ctx.enter_context(tc.tile_pool(name="ring", bufs=2))
         psum = ctx.enter_context(tc.psum_pool(name="psum", bufs=2))
 
-        v_runs = [(0, 768, 0), (0, 512, 1), (0, 512, 2)]
-        s_runs = [(768, 768, 0), (512, 1024, 1), (512, 1024, 2), (1536, 1024, 0), (1536, 1024, 1), (1536, 1024, 2), (2560, 512, 0), (2560, 512, 1), (2560, 256, 2), (2816, 128, 2), (2944, 128, 2)]
-        v_slots = max(r[0] + r[1] for r in v_runs)
+        v_runs = [(0, 512, 0), (2560, 256, 0), (0, 512, 1), (0, 512, 2)]
+        s_runs = [(512, 1024, 0), (512, 1024, 1), (512, 1024, 2), (1536, 1024, 0), (1536, 1024, 1), (1536, 1024, 2), (2816, 256, 0), (2560, 512, 1), (2560, 256, 2), (2816, 128, 2), (2944, 128, 2)]
 
-        def pieces(run):
-            first, count, a = run
-            cuts = sorted({first, first + count} | {b for b in range(0, S, BANK) if first < b < first + count})
-            return [(lo, hi - lo, a) for lo, hi in zip(cuts, cuts[1:])]
+        def cut(first, count, step):
+            edges = sorted({first, first + count} | {b for b in range(0, S, step) if first < b < first + count})
+            return [(lo, hi - lo) for lo, hi in zip(edges, edges[1:])]
 
         offs_sb = keep.tile([P, S // 16], U16, name="offs_sb")
         dy_rows = dyT.rearrange("(a p t) x -> a t p x", p=P, t=PACK)
         dy = [[keep.tile([P, WINDOW], F32, name=f"dy{a}_{t}") for t in range(PACK)] for a in range(PASSES)]
-        gate_v = keep.tile([P, v_slots], F32, name="gate_v")
-        gate_rows = keep.tile([P, P], F32, name="gate_rows")
+        gate_v = {}
 
+        def load_gate(run):
+            if run[:2] not in gate_v:
+                gate_v[run[:2]] = keep.tile([P, run[1]], F32, name=f"gate_v{run[0]}")
+                nc.sync.dma_start(gate_v[run[:2]][:], gate[0:P, run[0]:run[0] + run[1]])
+
+        gate_rows = keep.tile([P, P], F32, name="gate_rows")
         nc.sync.dma_start(offs_sb[:], offs)
         nc.sync.dma_start(dy[0][0][:, 0:T], dy_rows[0, 0])
-        nc.sync.dma_start(gate_v[:], gate[0:P, 0:v_slots])
+        load_gate(v_runs[0])
         for t in range(1, PACK):
             nc.sync.dma_start(dy[0][t][:, 0:T], dy_rows[0, t])
+        for run in v_runs[1:]:
+            load_gate(run)
         nc.sync.dma_start(gate_rows[:], gate.rearrange("r (m q) -> (r m) q", q=P)[0:P, :])
         for a in range(1, PASSES):
             for t in range(PACK):
@@ -67,7 +73,7 @@ def tile_moe_bdx_lin_none_kernel(tc, dyT, w, gate, offs, pos1, pos2, pos3, pos4,
 
         ident = keep.tile([P, P], F32, name="ident")
         make_identity(nc, ident[:])
-        turned = psum.tile([P, P], F32, name="turned", tag="acc", bufs=5)
+        turned = psum.tile([P, P], F32, name="turned", tag="acc", bufs=4)
         nc.tensor.transpose(turned[:], gate_rows[:], ident[:])
         gate_cols = keep.tile([P, S // P], F32, name="gate_cols")
         nc.vector.tensor_copy(gate_cols[:], turned[:, 0:S // P])
@@ -76,7 +82,7 @@ def tile_moe_bdx_lin_none_kernel(tc, dyT, w, gate, offs, pos1, pos2, pos3, pos4,
         gate_ps, planes, g_bf, g_mx, w_raw, w_bf, w_mx, acc = {}, {}, {}, {}, {}, {}, {}, {}
 
         def spread_gate(c):
-            gate_ps[c] = psum.tile([P, BANK], F32, name="gate_bank", bufs=3)
+            gate_ps[c] = psum.tile([P, BANK], F32, name="gate_bank", bufs=4)
             for b in range(BANK // P):
                 m = c * (BANK // P) + b
                 nc.tensor.transpose(gate_ps[c][:, b * P:(b + 1) * P], gate_cols[:, m:m + 1].to_broadcast([P, P]), ident[:])
@@ -84,70 +90,69 @@ def tile_moe_bdx_lin_none_kernel(tc, dyT, w, gate, offs, pos1, pos2, pos3, pos4,
         def offsets(run):
             return offs_sb[:, run[0] // 16:(run[0] + run[1]) // 16]
 
-        def hand_on(run, tile):
-            for piece in pieces(run):
-                planes[piece] = tile[:, :, piece[0] - run[0]:piece[0] - run[0] + piece[1]]
-
         def gather_scalar(run):
-            tile = ring.tile([P, PACK, run[1]], F32, name="planes_s", tag="planes_s", bufs=PLANE_BUFS)
+            planes[run] = ring.tile([P, PACK, run[1]], F32, name="planes_s", tag="planes_s", bufs=PLANE_BUFS)
             for t in range(PACK):
-                nc.scalar.activation(tile[:, t, :], dy[run[2]][t][:].indirect(offsets(run)), COPY)
-            hand_on(run, tile)
+                nc.scalar.activation(planes[run][:, t, :], dy[run[2]][t][:].indirect(offsets(run)), COPY)
 
         def gather_vector(run):
-            tile = ring.tile([P, PACK, run[1]], F32, name="planes_v", bufs=2)
+            planes[run] = ring.tile([P, PACK, run[1]], F32, name="planes_v", bufs=2)
             for t in range(PACK):
-                nc.vector.tensor_tensor(tile[:, t, :], dy[run[2]][t][:].indirect(offsets(run)),
-                                        gate_v[:, run[0]:run[0] + run[1]], MULT)
-            hand_on(run, tile)
+                nc.vector.tensor_tensor(planes[run][:, t, :], dy[run[2]][t][:].indirect(offsets(run)),
+                                        gate_v[run[:2]][:], MULT)
 
-        def weave(piece, tag, bufs):
-            g_bf[piece] = ring.tile([P, piece[1], PACK], BF16, name=tag, tag=tag, bufs=bufs, align_bytes=64)
+        def weave(run, tag, bufs):
+            g_bf[run] = ring.tile([P, run[1], PACK], BF16, name=tag, tag=tag, bufs=bufs, align_bytes=64)
             nc.vector.tensor_copy(
-                g_bf[piece][:].rearrange("p (x i) t -> p x t i", i=4),
-                planes[piece].rearrange("p t (x i) -> p x t i", i=4))
+                g_bf[run][:].rearrange("p (x i) t -> p x t i", i=4),
+                planes[run][:].rearrange("p t (x i) -> p x t i", i=4))
 
-        def gate_and_weave(piece):
-            first, count, a = piece
-            g_bf[piece] = ring.tile([P, count, PACK], BF16, name="g_bf", tag="g_bf", bufs=3, align_bytes=64)
-            gates = gate_ps[first // BANK][:, first % BANK:first % BANK + count]
-            nc.vector.tensor_tensor(
-                g_bf[piece][:].rearrange("p (x i) t -> p x t i", i=2),
-                planes[piece].rearrange("p t (x i) -> p x t i", i=2),
-                gates.rearrange("p (x i) -> p x i", i=2).unsqueeze(2).to_broadcast([P, count // 2, PACK, 2]),
-                MULT)
+        def gate_and_weave(run):
+            g_bf[run] = ring.tile([P, run[1], PACK], BF16, name="g_bf", tag="g_bf", bufs=2, align_bytes=64)
+            for first, count in cut(run[0], run[1], BANK):
+                cols = slice(first - run[0], first - run[0] + count)
+                gates = gate_ps[first // BANK][:, first % BANK:first % BANK + count]
+                nc.vector.tensor_tensor(
+                    g_bf[run][:, cols, :].rearrange("p (x i) t -> p x t i", i=2),
+                    planes[run][:, :, cols].rearrange("p t (x i) -> p x t i", i=2),
+                    gates.rearrange("p (x i) -> p x i", i=2).unsqueeze(2).to_broadcast([P, count // 2, PACK, 2]),
+                    MULT)
 
-        def quantize_g(piece):
-            first, count, a = piece
-            codes = ring.tile([P, count], U32, name="g_codes", bufs=G_BUFS, align_bytes=64)
-            scales = ring.tile([P, count], U8, name="g_scales", bufs=G_BUFS, align_bytes=64)
+        def quantize_g(run, tag, bufs):
+            first, count, a = run
+            codes = ring.tile([P, count], U32, name=tag + "_codes", bufs=bufs, align_bytes=64)
+            scales = ring.tile([P, count], U8, name=tag + "_scales", bufs=bufs, align_bytes=64)
             nc.vector.quantize_mx(out=codes[:].bitcast(FP8X4), scales=scales[:],
-                                  in_=g_bf[piece][:].rearrange("p x t -> p (x t)"))
-            for lo in range(0, count, C):
-                hi = min(lo + C, count)
-                g_mx.setdefault(((first + lo) // C, a), []).append((codes[:, lo:hi], scales[:, lo:hi], (first + lo) % C, hi - lo))
+                                  in_=g_bf[run][:].rearrange("p x t -> p (x t)"))
+            for lo, size in cut(first, count, C):
+                cols = slice(lo - first, lo - first + size)
+                g_mx.setdefault((lo // C, a), []).append((codes[:, cols], scales[:, cols], lo % C, size))
 
-        def load_w(e):
-            w_raw[e] = ring.tile([P, PASSES, PACK, K], F32, name="w_raw", bufs=W_BUFS)
-            nc.sync.dma_start(w_raw[e][:], w[e].rearrange("(a p j) k -> p a j k", p=P, j=PACK))
+        def load_w(q):
+            w_raw[q] = ring.tile([P, 2 * PASSES, PACK, K], F32, name="w_raw", bufs=W_BUFS)
+            nc.sync.dma_start(w_raw[q][:], w[2 * q:2 * q + 2].rearrange("e (a p j) k -> p (e a) j k", p=P, j=PACK))
 
-        def weave_w(e):
-            w_bf[e] = ring.tile([P, PASSES, K, PACK], BF16, name="w_bf", tag="w_bf", bufs=1, align_bytes=64)
-            nc.gpsimd.tensor_scalar(w_bf[e][:], w_raw[e][:].rearrange("p a j k -> p a k j"), 1.0, 0.0, MULT, ADD)
+        def weave_w(q):
+            w_bf[q] = ring.tile([P, 2 * PASSES, K, PACK], BF16, name="w_bf", tag="w_bf", bufs=1, align_bytes=64)
+            nc.gpsimd.tensor_scalar(w_bf[q][:], w_raw[q][:].rearrange("p a j k -> p a k j"), 1.0, 0.0, MULT, ADD)
 
-        def quantize_w(e):
-            codes = ring.tile([P, PASSES * K], U32, name="w_codes", bufs=5, align_bytes=64)
-            scales = ring.tile([P, PASSES * K], U8, name="w_scales", bufs=5, align_bytes=64)
-            nc.vector.quantize_mx(out=codes[:].bitcast(FP8X4), scales=scales[:],
-                                  in_=w_bf[e][:].rearrange("p a k j -> p (a k j)"))
-            w_mx[e] = (codes, scales)
+        def quantize_w(q):
+            codes = ring.tile([P, 2 * PASSES * K], U32, name="w_codes", bufs=3, align_bytes=64)
+            scales = ring.tile([P, 2 * PASSES * K], U8, name="w_scales", bufs=3, align_bytes=64)
+            flat = w_bf[q][:].rearrange("p a k j -> p (a k j)")
+            for lo, hi in ((0, 512), (512, 768)):
+                nc.vector.quantize_mx(out=codes[:, lo:hi].bitcast(FP8X4), scales=scales[:, lo:hi],
+                                      in_=flat[:, PACK * lo:PACK * hi])
+            for h in range(2):
+                cols = slice(h * PASSES * K, (h + 1) * PASSES * K)
+                w_mx[2 * q + h] = (codes[:, cols], scales[:, cols])
 
         def quantized(e, a):
-            return sum(part[3] for part in g_mx.get((e, a), [])) == C
+            return e in w_mx and sum(part[3] for part in g_mx.get((e, a), [])) == C
 
         def multiply(e, a):
             if a == 0:
-                acc[e] = psum.tile([P, C], F32, name="acc", tag="acc", bufs=5)
+                acc[e] = psum.tile([P, C], F32, name="acc", tag="acc", bufs=4)
             parts = g_mx[e, a]
             for i, (codes, scales, lo, count) in enumerate(parts):
                 nc.tensor.matmul_mx(
@@ -156,62 +161,63 @@ def tile_moe_bdx_lin_none_kernel(tc, dyT, w, gate, offs, pos1, pos2, pos3, pos4,
                     lhsT_scale=w_mx[e][1][:, a * K:(a + 1) * K],
                     rhs=codes.bitcast(FP8X4),
                     rhs_scale=scales,
-                    start=(a == 0), stop=(a == PASSES - 1 and i == len(parts) - 1))
+                    start=(a == 0 and i == 0), stop=(a == PASSES - 1 and i == len(parts) - 1))
             if a == PASSES - 1:
-                if False:
+                if e < 4:
                     nc.vector.tensor_copy(dx[:, e * C:(e + 1) * C], acc[e][:])
                 else:
                     nc.scalar.copy(dx[:, e * C:(e + 1) * C], acc[e][:])
 
-        s_pieces = [piece for run in s_runs for piece in pieces(run)]
-        v_pieces = [piece for run in v_runs for piece in pieces(run)]
-        s_banks = sorted({piece[0] // BANK for piece in s_pieces})
+        passes_done = [0] * E
 
-        for e in range(W_BUFS):
-            load_w(e)
-        for c in s_banks[:2]:
-            spread_gate(c)
+        def multiply_ready():
+            for e in range(E):
+                if e >= E - 2 or all(quantized(e, a) for a in range(PASSES)):
+                    while passes_done[e] < PASSES and quantized(e, passes_done[e]):
+                        multiply(e, passes_done[e])
+                        passes_done[e] += 1
+
+        def spread_for(run):
+            for first, count in cut(run[0], run[1], BANK):
+                if first // BANK not in gate_ps:
+                    spread_gate(first // BANK)
+
+        for q in range(W_BUFS):
+            load_w(q)
+        spread_for(s_runs[0])
         for run in s_runs[:PLANE_BUFS - 1]:
             gather_scalar(run)
         gather_vector(v_runs[0])
         for i, run in enumerate(v_runs):
             if i + 1 < len(v_runs):
                 gather_vector(v_runs[i + 1])
-            for piece in pieces(run):
-                if piece == v_pieces[-1]:
-                    weave(piece, "w_bf", 1)
-                else:
-                    weave(piece, "g_bf", 3)
+                weave(run, "g_bf", 2)
+            else:
+                weave(run, "w_bf", 1)
             if i >= 1:
-                for piece in pieces(v_runs[i - 1]):
-                    quantize_g(piece)
-        for piece in pieces(v_runs[-1]):
-            quantize_g(piece)
+                quantize_g(v_runs[i - 1], "gv", len(v_runs))
+        quantize_g(v_runs[-1], "gv", len(v_runs))
+        weave_w(0)
+        load_w(W_BUFS)
 
-        passes_done = [0] * E
-        gathered = PLANE_BUFS - 1
-        starts = [pieces(run)[0] for run in s_runs]
-        for s in range(len(s_pieces) + 2):
-            if s < len(s_pieces):
-                if s_pieces[s] in starts and gathered < len(s_runs):
-                    gather_scalar(s_runs[gathered])
-                    gathered += 1
-                for piece in s_pieces[s:s + 3]:
-                    if piece[0] // BANK not in gate_ps:
-                        spread_gate(piece[0] // BANK)
-                gate_and_weave(s_pieces[s])
-            for e in range(E):
-                while passes_done[e] < PASSES and e in w_mx and quantized(e, passes_done[e]) and (e < 4 or passes_done[e - 4] == PASSES):
-                    multiply(e, passes_done[e])
-                    passes_done[e] += 1
-            if 1 <= s <= len(s_pieces):
-                quantize_g(s_pieces[s - 1])
-            if 1 <= s <= E:
-                quantize_w(s - 1)
-            if s < E:
-                weave_w(s)
-                if s + W_BUFS < E:
-                    load_w(s + W_BUFS)
+        for s, run in enumerate(s_runs):
+            if s + PLANE_BUFS - 1 < len(s_runs):
+                gather_scalar(s_runs[s + PLANE_BUFS - 1])
+            if s + 1 < len(s_runs):
+                spread_for(s_runs[s + 1])
+            gate_and_weave(run)
+            multiply_ready()
+            if s < PAIRS:
+                quantize_w(s)
+                quantize_g(run, "gs", G_BUFS)
+            elif s > PAIRS:
+                quantize_g(s_runs[s - 1], "gs", G_BUFS)
+            if s + 1 < PAIRS:
+                weave_w(s + 1)
+                if s + 1 + W_BUFS < PAIRS:
+                    load_w(s + 1 + W_BUFS)
+        quantize_g(s_runs[-1], "gs", G_BUFS)
+        multiply_ready()
         assert passes_done == [PASSES] * E
 
         spare = ring.tile([P, 5, T], F32, name="spare", tag="planes_s", bufs=PLANE_BUFS)

@@ -22,11 +22,24 @@ P = 128
 PACK = 4
 PASSES = N // (P * PACK)
 BANK = 512
-WINDOW = 1040
+PER_COLUMN = 16
 PAIRS = E // 2
+
+V_RUNS = [(0, 2 * C, 0), (10 * C, C, 0), (0, 2 * C, 1), (0, 2 * C, 2)]
+S_RUNS = [(first, 4 * C, a) for first in (2 * C, 6 * C) for a in range(PASSES)] + [
+    (11 * C, C, 0), (10 * C, 2 * C, 1), (10 * C, C, 2), (11 * C, C // 2, 2), (11 * C + C // 2, C // 2, 2)]
+WINDOW = 4 * C + PER_COLUMN
+V_EXITS = 4
 PLANE_BUFS = 3
 W_BUFS = 2
 G_BUFS = 5
+ACC_BUFS = 4
+GATE_BUFS = 4
+
+
+def cut(first, count, step):
+    edges = sorted({first, first + count} | {b for b in range(0, S, step) if first < b < first + count})
+    return [(lo, hi - lo) for lo, hi in zip(edges, edges[1:])]
 
 
 def tile_moe_bdx_lin_none_kernel(tc, dyT, w, gate, offs, pos1, pos2, pos3, pos4, out):
@@ -36,14 +49,7 @@ def tile_moe_bdx_lin_none_kernel(tc, dyT, w, gate, offs, pos1, pos2, pos3, pos4,
         ring = ctx.enter_context(tc.tile_pool(name="ring", bufs=2))
         psum = ctx.enter_context(tc.psum_pool(name="psum", bufs=2))
 
-        v_runs = [(0, 512, 0), (2560, 256, 0), (0, 512, 1), (0, 512, 2)]
-        s_runs = [(512, 1024, 0), (512, 1024, 1), (512, 1024, 2), (1536, 1024, 0), (1536, 1024, 1), (1536, 1024, 2), (2816, 256, 0), (2560, 512, 1), (2560, 256, 2), (2816, 128, 2), (2944, 128, 2)]
-
-        def cut(first, count, step):
-            edges = sorted({first, first + count} | {b for b in range(0, S, step) if first < b < first + count})
-            return [(lo, hi - lo) for lo, hi in zip(edges, edges[1:])]
-
-        offs_sb = keep.tile([P, S // 16], U16, name="offs_sb")
+        offs_sb = keep.tile([P, S // PER_COLUMN], U16, name="offs_sb")
         dy_rows = dyT.rearrange("(a p t) x -> a t p x", p=P, t=PACK)
         dy = [[keep.tile([P, WINDOW], F32, name=f"dy{a}_{t}") for t in range(PACK)] for a in range(PASSES)]
         gate_v = {}
@@ -56,10 +62,10 @@ def tile_moe_bdx_lin_none_kernel(tc, dyT, w, gate, offs, pos1, pos2, pos3, pos4,
         gate_rows = keep.tile([P, P], F32, name="gate_rows")
         nc.sync.dma_start(offs_sb[:], offs)
         nc.sync.dma_start(dy[0][0][:, 0:T], dy_rows[0, 0])
-        load_gate(v_runs[0])
+        load_gate(V_RUNS[0])
         for t in range(1, PACK):
             nc.sync.dma_start(dy[0][t][:, 0:T], dy_rows[0, t])
-        for run in v_runs[1:]:
+        for run in V_RUNS[1:]:
             load_gate(run)
         nc.sync.dma_start(gate_rows[:], gate.rearrange("r (m q) -> (r m) q", q=P)[0:P, :])
         for a in range(1, PASSES):
@@ -67,13 +73,13 @@ def tile_moe_bdx_lin_none_kernel(tc, dyT, w, gate, offs, pos1, pos2, pos3, pos4,
                 nc.sync.dma_start(dy[a][t][:, 0:T], dy_rows[a, t])
         pos_sb = []
         for r, pos in enumerate((pos1, pos2, pos3, pos4)):
-            pos_tile = keep.tile([P, T // 16], U16, name=f"pos_sb{r}")
+            pos_tile = keep.tile([P, T // PER_COLUMN], U16, name=f"pos_sb{r}")
             nc.sync.dma_start(pos_tile[:], pos)
             pos_sb.append(pos_tile)
 
         ident = keep.tile([P, P], F32, name="ident")
         make_identity(nc, ident[:])
-        turned = psum.tile([P, P], F32, name="turned", tag="acc", bufs=4)
+        turned = psum.tile([P, P], F32, name="turned", tag="acc", bufs=ACC_BUFS)
         nc.tensor.transpose(turned[:], gate_rows[:], ident[:])
         gate_cols = keep.tile([P, S // P], F32, name="gate_cols")
         nc.vector.tensor_copy(gate_cols[:], turned[:, 0:S // P])
@@ -82,13 +88,18 @@ def tile_moe_bdx_lin_none_kernel(tc, dyT, w, gate, offs, pos1, pos2, pos3, pos4,
         gate_ps, planes, g_bf, g_mx, w_raw, w_bf, w_mx, acc = {}, {}, {}, {}, {}, {}, {}, {}
 
         def spread_gate(c):
-            gate_ps[c] = psum.tile([P, BANK], F32, name="gate_bank", bufs=4)
+            gate_ps[c] = psum.tile([P, BANK], F32, name="gate_bank", bufs=GATE_BUFS)
             for b in range(BANK // P):
                 m = c * (BANK // P) + b
                 nc.tensor.transpose(gate_ps[c][:, b * P:(b + 1) * P], gate_cols[:, m:m + 1].to_broadcast([P, P]), ident[:])
 
+        def spread_for(run):
+            for first, count in cut(run[0], run[1], BANK):
+                if first // BANK not in gate_ps:
+                    spread_gate(first // BANK)
+
         def offsets(run):
-            return offs_sb[:, run[0] // 16:(run[0] + run[1]) // 16]
+            return offs_sb[:, run[0] // PER_COLUMN:(run[0] + run[1]) // PER_COLUMN]
 
         def gather_scalar(run):
             planes[run] = ring.tile([P, PACK, run[1]], F32, name="planes_s", tag="planes_s", bufs=PLANE_BUFS)
@@ -130,17 +141,17 @@ def tile_moe_bdx_lin_none_kernel(tc, dyT, w, gate, offs, pos1, pos2, pos3, pos4,
 
         def load_w(q):
             w_raw[q] = ring.tile([P, 2 * PASSES, PACK, K], F32, name="w_raw", bufs=W_BUFS)
-            nc.sync.dma_start(w_raw[q][:], w[2 * q:2 * q + 2].rearrange("e (a p j) k -> p (e a) j k", p=P, j=PACK))
+            nc.sync.dma_start(w_raw[q][:], w[2 * q:2 * q + 2].rearrange("e (a p t) k -> p (e a) t k", p=P, t=PACK))
 
         def weave_w(q):
             w_bf[q] = ring.tile([P, 2 * PASSES, K, PACK], BF16, name="w_bf", tag="w_bf", bufs=1, align_bytes=64)
-            nc.gpsimd.tensor_scalar(w_bf[q][:], w_raw[q][:].rearrange("p a j k -> p a k j"), 1.0, 0.0, MULT, ADD)
+            nc.gpsimd.tensor_scalar(w_bf[q][:], w_raw[q][:].rearrange("p a t k -> p a k t"), 1.0, 0.0, MULT, ADD)
 
         def quantize_w(q):
             codes = ring.tile([P, 2 * PASSES * K], U32, name="w_codes", bufs=3, align_bytes=64)
             scales = ring.tile([P, 2 * PASSES * K], U8, name="w_scales", bufs=3, align_bytes=64)
-            flat = w_bf[q][:].rearrange("p a k j -> p (a k j)")
-            for lo, hi in ((0, 512), (512, 768)):
+            flat = w_bf[q][:].rearrange("p a k t -> p (a k t)")
+            for lo, hi in ((0, 512), (512, 2 * PASSES * K)):
                 nc.vector.quantize_mx(out=codes[:, lo:hi].bitcast(FP8X4), scales=scales[:, lo:hi],
                                       in_=flat[:, PACK * lo:PACK * hi])
             for h in range(2):
@@ -152,7 +163,7 @@ def tile_moe_bdx_lin_none_kernel(tc, dyT, w, gate, offs, pos1, pos2, pos3, pos4,
 
         def multiply(e, a):
             if a == 0:
-                acc[e] = psum.tile([P, C], F32, name="acc", tag="acc", bufs=4)
+                acc[e] = psum.tile([P, C], F32, name="acc", tag="acc", bufs=ACC_BUFS)
             parts = g_mx[e, a]
             for i, (codes, scales, lo, count) in enumerate(parts):
                 nc.tensor.matmul_mx(
@@ -163,7 +174,7 @@ def tile_moe_bdx_lin_none_kernel(tc, dyT, w, gate, offs, pos1, pos2, pos3, pos4,
                     rhs_scale=scales,
                     start=(a == 0 and i == 0), stop=(a == PASSES - 1 and i == len(parts) - 1))
             if a == PASSES - 1:
-                if e < 4:
+                if e < V_EXITS:
                     nc.vector.tensor_copy(dx[:, e * C:(e + 1) * C], acc[e][:])
                 else:
                     nc.scalar.copy(dx[:, e * C:(e + 1) * C], acc[e][:])
@@ -177,66 +188,65 @@ def tile_moe_bdx_lin_none_kernel(tc, dyT, w, gate, offs, pos1, pos2, pos3, pos4,
                         multiply(e, passes_done[e])
                         passes_done[e] += 1
 
-        def spread_for(run):
-            for first, count in cut(run[0], run[1], BANK):
-                if first // BANK not in gate_ps:
-                    spread_gate(first // BANK)
-
         for q in range(W_BUFS):
             load_w(q)
-        spread_for(s_runs[0])
-        for run in s_runs[:PLANE_BUFS - 1]:
+        spread_for(S_RUNS[0])
+        for run in S_RUNS[:PLANE_BUFS - 1]:
             gather_scalar(run)
-        gather_vector(v_runs[0])
-        for i, run in enumerate(v_runs):
-            if i + 1 < len(v_runs):
-                gather_vector(v_runs[i + 1])
+        gather_vector(V_RUNS[0])
+        for i, run in enumerate(V_RUNS):
+            if i + 1 < len(V_RUNS):
+                gather_vector(V_RUNS[i + 1])
                 weave(run, "g_bf", 2)
             else:
                 weave(run, "w_bf", 1)
             if i >= 1:
-                quantize_g(v_runs[i - 1], "gv", len(v_runs))
-        quantize_g(v_runs[-1], "gv", len(v_runs))
+                quantize_g(V_RUNS[i - 1], "gv", len(V_RUNS))
+        quantize_g(V_RUNS[-1], "gv", len(V_RUNS))
         weave_w(0)
         load_w(W_BUFS)
 
-        for s, run in enumerate(s_runs):
-            if s + PLANE_BUFS - 1 < len(s_runs):
-                gather_scalar(s_runs[s + PLANE_BUFS - 1])
-            if s + 1 < len(s_runs):
-                spread_for(s_runs[s + 1])
+        for s, run in enumerate(S_RUNS):
+            if s + PLANE_BUFS - 1 < len(S_RUNS):
+                gather_scalar(S_RUNS[s + PLANE_BUFS - 1])
+            if s + 1 < len(S_RUNS):
+                spread_for(S_RUNS[s + 1])
             gate_and_weave(run)
             multiply_ready()
             if s < PAIRS:
                 quantize_w(s)
                 quantize_g(run, "gs", G_BUFS)
             elif s > PAIRS:
-                quantize_g(s_runs[s - 1], "gs", G_BUFS)
+                quantize_g(S_RUNS[s - 1], "gs", G_BUFS)
             if s + 1 < PAIRS:
                 weave_w(s + 1)
                 if s + 1 + W_BUFS < PAIRS:
                     load_w(s + 1 + W_BUFS)
-        quantize_g(s_runs[-1], "gs", G_BUFS)
+        quantize_g(S_RUNS[-1], "gs", G_BUFS)
         multiply_ready()
         assert passes_done == [PASSES] * E
 
         spare = ring.tile([P, 5, T], F32, name="spare", tag="planes_s", bufs=PLANE_BUFS)
-        first, second, two, three, four = (spare[:, j, :] for j in range(5))
+        by_pos1, by_pos2, two, three, total = (spare[:, j, :] for j in range(5))
+        by_pos4 = ring.tile([P, T], F32, name="planes_v", bufs=2)
+        low, mid, high = (slice(i * T // 3, (i + 1) * T // 3) for i in range(3))
+        both = slice(low.start, mid.stop)
 
-        def picked(r, lo, hi):
-            return dx[:].indirect(pos_sb[r][:, lo // 16:hi // 16])
+        def picked(r, tokens):
+            return dx[:].indirect(pos_sb[r][:, tokens.start // PER_COLUMN:tokens.stop // PER_COLUMN])
 
-        cuts = [(0, 128), (128, 384), (384, T)]
-        halves = [(0, 384), (384, T)]
-        for lo, hi in cuts:
-            nc.scalar.activation(first[:, lo:hi], picked(0, lo, hi), COPY)
-        for lo, hi in halves:
-            nc.scalar.activation(second[:, lo:hi], picked(1, lo, hi), COPY)
-        for kind, (lo, hi) in [(2, cuts[0]), (3, cuts[0]), (2, cuts[1]), (2, cuts[2]), (3, cuts[1]), (3, cuts[2])]:
-            if kind == 2:
-                nc.vector.tensor_tensor(two[:, lo:hi], picked(2, lo, hi), first[:, lo:hi], ADD)
-            else:
-                nc.vector.tensor_tensor(three[:, lo:hi], picked(3, lo, hi), two[:, lo:hi], ADD)
-        for lo, hi in halves:
-            nc.vector.tensor_tensor(four[:, lo:hi], three[:, lo:hi], second[:, lo:hi], ADD)
-            nc.sync.dma_start(out[:, lo:hi], four[:, lo:hi])
+        for tokens in (low, mid, high):
+            nc.scalar.activation(by_pos1[:, tokens], picked(0, tokens), COPY)
+        nc.scalar.activation(by_pos2[:, both], picked(1, both), COPY)
+        nc.scalar.activation(by_pos4[:, high], picked(3, high), COPY)
+        nc.scalar.activation(by_pos2[:, high], picked(1, high), COPY)
+        nc.vector.tensor_copy(by_pos4[:, low], picked(3, low))
+        nc.vector.tensor_tensor(two[:, low], picked(2, low), by_pos1[:, low], ADD)
+        nc.vector.tensor_tensor(two[:, mid], picked(2, mid), by_pos1[:, mid], ADD)
+        nc.vector.tensor_tensor(three[:, low], by_pos4[:, low], two[:, low], ADD)
+        nc.vector.tensor_tensor(two[:, high], picked(2, high), by_pos1[:, high], ADD)
+        nc.vector.tensor_tensor(three[:, mid], picked(3, mid), two[:, mid], ADD)
+        nc.vector.tensor_tensor(three[:, high], by_pos4[:, high], two[:, high], ADD)
+        for tokens in (both, high):
+            nc.vector.tensor_tensor(total[:, tokens], three[:, tokens], by_pos2[:, tokens], ADD)
+            nc.sync.dma_start(out[:, tokens], total[:, tokens])

from contextlib import ExitStack

import concourse.mybir as mybir
from concourse.masks import make_identity

K, T, E, C, N = 128, 768, 12, 256, 1536
S = E * C
FLOPS = 2 * S * N * K
BYTES = 4 * (N * T + E * N * K + S + K * T) + 2 * 128 * (S + 4 * T) // 16

F32 = mybir.dt.float32
BF16 = mybir.dt.bfloat16
U32 = mybir.dt.uint32
U16 = mybir.dt.uint16
U8 = mybir.dt.uint8
FP8X4 = mybir.dt.float8_e4m3fn_x4
MULT = mybir.AluOpType.mult
ADD = mybir.AluOpType.add
COPY = mybir.ActivationFunctionType.Copy

P = 128
PACK = 4
PASSES = N // (P * PACK)
BANK = 512
PER_COLUMN = 16
PAIRS = E // 2

V_RUNS = [(0, 2 * C, 0), (10 * C, C, 0), (0, 2 * C, 1), (0, 2 * C, 2)]
S_RUNS = [(first, 4 * C, a) for first in (2 * C, 6 * C) for a in range(PASSES)] + [
    (11 * C, C, 0), (10 * C, 2 * C, 1), (10 * C, C, 2), (11 * C, C // 2, 2), (11 * C + C // 2, C // 2, 2)]
WINDOW = 4 * C + PER_COLUMN
V_EXITS = 4
PLANE_BUFS = 3
W_BUFS = 2
G_BUFS = 5
ACC_BUFS = 4
GATE_BUFS = 4


def cut(first, count, step):
    edges = sorted({first, first + count} | {b for b in range(0, S, step) if first < b < first + count})
    return [(lo, hi - lo) for lo, hi in zip(edges, edges[1:])]


def tile_moe_bdx_lin_none_kernel(tc, dyT, w, gate, offs, pos1, pos2, pos3, pos4, out):
    nc = tc.nc
    with ExitStack() as ctx:
        keep = ctx.enter_context(tc.tile_pool(name="keep", bufs=1))
        ring = ctx.enter_context(tc.tile_pool(name="ring", bufs=2))
        psum = ctx.enter_context(tc.psum_pool(name="psum", bufs=2))

        offs_sb = keep.tile([P, S // PER_COLUMN], U16, name="offs_sb")
        dy_rows = dyT.rearrange("(a p t) x -> a t p x", p=P, t=PACK)
        dy = [[keep.tile([P, WINDOW], F32, name=f"dy{a}_{t}") for t in range(PACK)] for a in range(PASSES)]
        gate_v = {}

        def load_gate(run):
            if run[:2] not in gate_v:
                gate_v[run[:2]] = keep.tile([P, run[1]], F32, name=f"gate_v{run[0]}")
                nc.sync.dma_start(gate_v[run[:2]][:], gate[0:P, run[0]:run[0] + run[1]])

        gate_rows = keep.tile([P, P], F32, name="gate_rows")
        nc.sync.dma_start(offs_sb[:], offs)
        nc.sync.dma_start(dy[0][0][:, 0:T], dy_rows[0, 0])
        load_gate(V_RUNS[0])
        for t in range(1, PACK):
            nc.sync.dma_start(dy[0][t][:, 0:T], dy_rows[0, t])
        for run in V_RUNS[1:]:
            load_gate(run)
        nc.sync.dma_start(gate_rows[:], gate.rearrange("r (m q) -> (r m) q", q=P)[0:P, :])
        for a in range(1, PASSES):
            for t in range(PACK):
                nc.sync.dma_start(dy[a][t][:, 0:T], dy_rows[a, t])
        pos_sb = []
        for r, pos in enumerate((pos1, pos2, pos3, pos4)):
            pos_tile = keep.tile([P, T // PER_COLUMN], U16, name=f"pos_sb{r}")
            nc.sync.dma_start(pos_tile[:], pos)
            pos_sb.append(pos_tile)

        ident = keep.tile([P, P], F32, name="ident")
        make_identity(nc, ident[:])
        turned = psum.tile([P, P], F32, name="turned", tag="acc", bufs=ACC_BUFS)
        nc.tensor.transpose(turned[:], gate_rows[:], ident[:])
        gate_cols = keep.tile([P, S // P], F32, name="gate_cols")
        nc.vector.tensor_copy(gate_cols[:], turned[:, 0:S // P])

        dx = keep.tile([P, S], F32, name="dx")
        gate_ps, planes, g_bf, g_mx, w_raw, w_bf, w_mx, acc = {}, {}, {}, {}, {}, {}, {}, {}

        def spread_gate(c):
            gate_ps[c] = psum.tile([P, BANK], F32, name="gate_bank", bufs=GATE_BUFS)
            for b in range(BANK // P):
                m = c * (BANK // P) + b
                nc.tensor.transpose(gate_ps[c][:, b * P:(b + 1) * P], gate_cols[:, m:m + 1].to_broadcast([P, P]), ident[:])

        def spread_for(run):
            for first, count in cut(run[0], run[1], BANK):
                if first // BANK not in gate_ps:
                    spread_gate(first // BANK)

        def offsets(run):
            return offs_sb[:, run[0] // PER_COLUMN:(run[0] + run[1]) // PER_COLUMN]

        def gather_scalar(run):
            planes[run] = ring.tile([P, PACK, run[1]], F32, name="planes_s", tag="planes_s", bufs=PLANE_BUFS)
            for t in range(PACK):
                nc.scalar.activation(planes[run][:, t, :], dy[run[2]][t][:].indirect(offsets(run)), COPY)

        def gather_vector(run):
            planes[run] = ring.tile([P, PACK, run[1]], F32, name="planes_v", bufs=2)
            for t in range(PACK):
                nc.vector.tensor_tensor(planes[run][:, t, :], dy[run[2]][t][:].indirect(offsets(run)),
                                        gate_v[run[:2]][:], MULT)

        def weave(run, tag, bufs):
            g_bf[run] = ring.tile([P, run[1], PACK], BF16, name=tag, tag=tag, bufs=bufs, align_bytes=64)
            nc.vector.tensor_copy(
                g_bf[run][:].rearrange("p (x i) t -> p x t i", i=4),
                planes[run][:].rearrange("p t (x i) -> p x t i", i=4))

        def gate_and_weave(run):
            g_bf[run] = ring.tile([P, run[1], PACK], BF16, name="g_bf", tag="g_bf", bufs=2, align_bytes=64)
            for first, count in cut(run[0], run[1], BANK):
                cols = slice(first - run[0], first - run[0] + count)
                gates = gate_ps[first // BANK][:, first % BANK:first % BANK + count]
                nc.vector.tensor_tensor(
                    g_bf[run][:, cols, :].rearrange("p (x i) t -> p x t i", i=2),
                    planes[run][:, :, cols].rearrange("p t (x i) -> p x t i", i=2),
                    gates.rearrange("p (x i) -> p x i", i=2).unsqueeze(2).to_broadcast([P, count // 2, PACK, 2]),
                    MULT)

        def quantize_g(run, tag, bufs):
            first, count, a = run
            codes = ring.tile([P, count], U32, name=tag + "_codes", bufs=bufs, align_bytes=64)
            scales = ring.tile([P, count], U8, name=tag + "_scales", bufs=bufs, align_bytes=64)
            nc.vector.quantize_mx(out=codes[:].bitcast(FP8X4), scales=scales[:],
                                  in_=g_bf[run][:].rearrange("p x t -> p (x t)"))
            for lo, size in cut(first, count, C):
                cols = slice(lo - first, lo - first + size)
                g_mx.setdefault((lo // C, a), []).append((codes[:, cols], scales[:, cols], lo % C, size))

        def load_w(q):
            w_raw[q] = ring.tile([P, 2 * PASSES, PACK, K], F32, name="w_raw", bufs=W_BUFS)
            nc.sync.dma_start(w_raw[q][:], w[2 * q:2 * q + 2].rearrange("e (a p t) k -> p (e a) t k", p=P, t=PACK))

        def weave_w(q):
            w_bf[q] = ring.tile([P, 2 * PASSES, K, PACK], BF16, name="w_bf", tag="w_bf", bufs=1, align_bytes=64)
            nc.gpsimd.tensor_scalar(w_bf[q][:], w_raw[q][:].rearrange("p a t k -> p a k t"), 1.0, 0.0, MULT, ADD)

        def quantize_w(q):
            codes = ring.tile([P, 2 * PASSES * K], U32, name="w_codes", bufs=3, align_bytes=64)
            scales = ring.tile([P, 2 * PASSES * K], U8, name="w_scales", bufs=3, align_bytes=64)
            flat = w_bf[q][:].rearrange("p a k t -> p (a k t)")
            for lo, hi in ((0, 512), (512, 2 * PASSES * K)):
                nc.vector.quantize_mx(out=codes[:, lo:hi].bitcast(FP8X4), scales=scales[:, lo:hi],
                                      in_=flat[:, PACK * lo:PACK * hi])
            for h in range(2):
                cols = slice(h * PASSES * K, (h + 1) * PASSES * K)
                w_mx[2 * q + h] = (codes[:, cols], scales[:, cols])

        def quantized(e, a):
            return e in w_mx and sum(part[3] for part in g_mx.get((e, a), [])) == C

        def multiply(e, a):
            if a == 0:
                acc[e] = psum.tile([P, C], F32, name="acc", tag="acc", bufs=ACC_BUFS)
            parts = g_mx[e, a]
            for i, (codes, scales, lo, count) in enumerate(parts):
                nc.tensor.matmul_mx(
                    out=acc[e][:, lo:lo + count],
                    lhsT=w_mx[e][0][:, a * K:(a + 1) * K].bitcast(FP8X4),
                    lhsT_scale=w_mx[e][1][:, a * K:(a + 1) * K],
                    rhs=codes.bitcast(FP8X4),
                    rhs_scale=scales,
                    start=(a == 0 and i == 0), stop=(a == PASSES - 1 and i == len(parts) - 1))
            if a == PASSES - 1:
                if e < V_EXITS:
                    nc.vector.tensor_copy(dx[:, e * C:(e + 1) * C], acc[e][:])
                else:
                    nc.scalar.copy(dx[:, e * C:(e + 1) * C], acc[e][:])

        passes_done = [0] * E

        def multiply_ready():
            for e in range(E):
                if e >= E - 2 or all(quantized(e, a) for a in range(PASSES)):
                    while passes_done[e] < PASSES and quantized(e, passes_done[e]):
                        multiply(e, passes_done[e])
                        passes_done[e] += 1

        for q in range(W_BUFS):
            load_w(q)
        spread_for(S_RUNS[0])
        for run in S_RUNS[:PLANE_BUFS - 1]:
            gather_scalar(run)
        gather_vector(V_RUNS[0])
        for i, run in enumerate(V_RUNS):
            if i + 1 < len(V_RUNS):
                gather_vector(V_RUNS[i + 1])
                weave(run, "g_bf", 2)
            else:
                weave(run, "w_bf", 1)
            if i >= 1:
                quantize_g(V_RUNS[i - 1], "gv", len(V_RUNS))
        quantize_g(V_RUNS[-1], "gv", len(V_RUNS))
        weave_w(0)
        load_w(W_BUFS)

        for s, run in enumerate(S_RUNS):
            if s + PLANE_BUFS - 1 < len(S_RUNS):
                gather_scalar(S_RUNS[s + PLANE_BUFS - 1])
            if s + 1 < len(S_RUNS):
                spread_for(S_RUNS[s + 1])
            gate_and_weave(run)
            multiply_ready()
            if s < PAIRS:
                quantize_w(s)
                quantize_g(run, "gs", G_BUFS)
            elif s > PAIRS:
                quantize_g(S_RUNS[s - 1], "gs", G_BUFS)
            if s + 1 < PAIRS:
                weave_w(s + 1)
                if s + 1 + W_BUFS < PAIRS:
                    load_w(s + 1 + W_BUFS)
        quantize_g(S_RUNS[-1], "gs", G_BUFS)
        multiply_ready()
        assert passes_done == [PASSES] * E

        spare = ring.tile([P, 5, T], F32, name="spare", tag="planes_s", bufs=PLANE_BUFS)
        by_pos1, by_pos2, two, three, total = (spare[:, j, :] for j in range(5))
        by_pos4 = ring.tile([P, T], F32, name="planes_v", bufs=2)
        low, mid, high = (slice(i * T // 3, (i + 1) * T // 3) for i in range(3))
        both = slice(low.start, mid.stop)

        def picked(r, tokens):
            return dx[:].indirect(pos_sb[r][:, tokens.start // PER_COLUMN:tokens.stop // PER_COLUMN])

        for tokens in (low, mid, high):
            nc.scalar.activation(by_pos1[:, tokens], picked(0, tokens), COPY)
        nc.scalar.activation(by_pos2[:, both], picked(1, both), COPY)
        nc.scalar.activation(by_pos4[:, high], picked(3, high), COPY)
        nc.scalar.activation(by_pos2[:, high], picked(1, high), COPY)
        nc.vector.tensor_copy(by_pos4[:, low], picked(3, low))
        nc.vector.tensor_tensor(two[:, low], picked(2, low), by_pos1[:, low], ADD)
        nc.vector.tensor_tensor(two[:, mid], picked(2, mid), by_pos1[:, mid], ADD)
        nc.vector.tensor_tensor(three[:, low], by_pos4[:, low], two[:, low], ADD)
        nc.vector.tensor_tensor(two[:, high], picked(2, high), by_pos1[:, high], ADD)
        nc.vector.tensor_tensor(three[:, mid], picked(3, mid), two[:, mid], ADD)
        nc.vector.tensor_tensor(three[:, high], by_pos4[:, high], two[:, high], ADD)
        for tokens in (both, high):
            nc.vector.tensor_tensor(total[:, tokens], three[:, tokens], by_pos2[:, tokens], ADD)
            nc.sync.dma_start(out[:, tokens], total[:, tokens])
